import numpy as np
import ml_dtypes


def mxq(x, axis, fmt="e4m3"):
    dtype, down = {"e4m3": (ml_dtypes.float8_e4m3fn, 7), "e5m2": (ml_dtypes.float8_e5m2, 14)}[fmt]
    v = np.moveaxis(np.asarray(x, np.float32).astype(ml_dtypes.bfloat16).astype(np.float64), axis, -1)
    blocks = v.reshape(v.shape[:-1] + (-1, 32))
    amax = np.abs(blocks).max(-1, keepdims=True)
    byte = np.maximum(np.where(amax > 0, np.frexp(amax)[1] - 1 + 127, 0) - down, 1)
    scale = np.exp2(byte - 127.0)
    codes = (blocks / scale).astype(np.float32).astype(dtype).astype(np.float64)
    return np.moveaxis((codes * scale).reshape(v.shape), -1, axis)


WIDE = False


def mx_kscale(k):
    if not WIDE:
        return np.ones(k)
    levels = np.array([30, -30])
    if k % 512:
        return np.exp2(np.random.permutation(np.resize(levels, k // 32))).repeat(32)
    a = np.empty((k // 512, 16))
    for p in range(k // 512):
        a[p, :8] = np.random.permutation(np.resize(levels, 8))
        for g in range(8):
            far = levels[np.abs(levels - a[p, g]) >= 10]
            a[p, g + 8] = far[np.random.randint(len(far))]
    return np.exp2(a.ravel()).repeat(32)


BF16 = ml_dtypes.bfloat16


def bf(x):
    return np.asarray(x, np.float32).astype(BF16)


def f64(x):
    return np.asarray(x).astype(np.float64)


E2M1 = np.array([0.0, 0.5, 1.0, 1.5, 2.0, 3.0, 4.0, 6.0, -0.0, -0.5, -1.0, -1.5, -2.0, -3.0, -4.0, -6.0])


def pack_weight(w, fmt):
    k, n = w.shape
    w = f64(bf(w)).reshape(k // 32, 32, n)
    amax = np.abs(w).max(1)
    if fmt == "e4m3":
        byte = np.frexp(amax)[1] - 1 + 127 - 7
    else:
        mant, ex = np.frexp(amax / 6.0)
        byte = np.where(mant > 0.5, ex, ex - 1) + 127
    byte = np.clip(np.where(amax > 0, byte, 1), 1, 254)
    scaled = (w * np.exp2(127.0 - byte)[:, None, :]).reshape(k, n).astype(np.float32)
    by_word = np.ascontiguousarray(scaled.reshape(k // 512, 128, 4, n).transpose(0, 1, 3, 2))
    if fmt == "e4m3":
        words = by_word.astype(ml_dtypes.float8_e4m3fn).view(np.uint8)
    else:
        c = by_word.astype(ml_dtypes.float4_e2m1fn).view(np.uint8) & 0xF
        words = c[..., 0::2] | (c[..., 1::2] << 4)
    return np.ascontiguousarray(words), np.ascontiguousarray(byte.astype(np.uint8).reshape(k // 512, 16, n))


def unpack_weight(words, scales, fmt):
    g, p, n, _ = words.shape
    if fmt == "e4m3":
        vals = np.ascontiguousarray(words).view(ml_dtypes.float8_e4m3fn).astype(np.float64)
    else:
        nib = np.empty((g, p, n, 4), np.uint8)
        nib[..., 0::2] = words & 0xF
        nib[..., 1::2] = words >> 4
        vals = E2M1[nib]
    vals = vals * np.repeat(np.exp2(scales.astype(np.float64) - 127.0), 8, axis=1)[..., None]
    return vals.transpose(0, 1, 3, 2).reshape(g * 512, n)
def pack4(w):
    words, scales = pack_weight(w, "e2m1")
    return words.reshape(words.shape[0], 128, -1), scales


def unpack4(words, scales):
    return unpack_weight(words.reshape(words.shape[0], 128, -1, 2), scales, "e2m1")


M, K, N = 1024, 2048, 1024


def setup_inputs():
    s = mx_kscale(K)
    t = mx_kscale(N)
    e = np.random.standard_normal((K, N)) / np.sqrt(K)
    basis_words, basis_scales = pack4(e / s[:, None] * t)
    return {"grad": bf(np.random.standard_normal((M, K)) * s),
            "basis_words": basis_words,
            "basis_scales": basis_scales,
            "lam": bf(np.exp(0.5 * np.random.standard_normal(N))),
            "mu": bf(0.25 + 0.5 * np.random.random(M)),
            "radius": bf(np.exp(0.2 * np.random.standard_normal(N)) * t),
            "back": bf(e.T / t[:, None])}


def reference(grad, basis_words, basis_scales, lam, mu, radius, back):
    c = mxq(f64(grad), 1, "e4m3") @ unpack4(basis_words, basis_scales)
    y = c / (f64(lam)[None, :] + f64(mu)[:, None])
    r = f64(radius)[None, :]
    z = np.minimum(np.maximum(y, -r), r)
    return -(mxq(z, 1, "e5m2") @ mxq(f64(back), 0, "e4m3"))

@@ -1,0 +1,368 @@
+from contextlib import ExitStack
+
+import concourse.mybir as mybir
+from concourse.masks import make_identity
+
+M, K, N = 1024, 2048, 1024
+FLOPS = 2 * M * K * N * 2
+
+F32 = mybir.dt.float32
+BF16 = mybir.dt.bfloat16
+I32 = mybir.dt.int32
+U32 = mybir.dt.uint32
+U8 = mybir.dt.uint8
+E4M3X4 = mybir.dt.float8_e4m3fn_x4
+E5M2X4 = mybir.dt.float8_e5m2_x4
+E2M1X4 = mybir.dt.float4_e2m1fn_x4
+ACT = mybir.ActivationFunctionType
+ALU = mybir.AluOpType
+
+P = 128
+W = 512
+
+
+def tile_trust_region_step_s9_kernel(tc, grad, basis_words, basis_scales, lam, mu, radius, back, out):
+    nc = tc.nc
+    with ExitStack() as ctx:
+        sb = ctx.enter_context(tc.tile_pool(name="sb", bufs=1))
+        ps = ctx.enter_context(tc.psum_pool(name="ps", bufs=1))
+        ctx.enter_context(tc.manual_schedule())
+
+        def keep(name, shape, dtype):
+            return sb.tile(shape, dtype, name=name, tag=name, align_bytes=64)
+
+        def bank(b, shape, dtype):
+            return ps.tile(shape, dtype, name="bank%d" % b, tag="bank%d" % b)
+
+        vec_rows = keep("vec_rows", [P, 2 * P], BF16)
+        scale_raw = keep("scale_raw", [P, 4, N], U8)
+        mu_col = keep("mu_col", [P, 8], BF16)
+        ident_b = keep("ident_b", [P, P], BF16)
+        ident_f = keep("ident_f", [P, P], F32)
+        nc.vector.memset(vec_rows[:], 0.0)
+        nc.vector.memset(scale_raw[:].bitcast(I32), 0)
+        make_identity(nc, ident_f[:])
+        nc.vector.tensor_copy(out=ident_b[:], in_=ident_f[:])
+
+        grad_v = grad.rearrange("(p m) k -> p m k", m=8)
+        out_v = out.rearrange("(p m) k -> p m k", m=8)
+        words_v = basis_words.bitcast(I32).rearrange("g p w -> p g w")
+        back_v = back.rearrange("(g a t r) k -> g r a t k", g=2, t=4, r=4)
+        grad_raw, e_raw, back_raw = {}, {}, {}
+
+        def load_grad(h, g):
+            grad_raw[h, g] = sb.tile([P, 4, W], BF16, name="grad_raw", tag="grad_raw", bufs=6, align_bytes=64)
+            nc.sync.dma_start(out=grad_raw[h, g][:], in_=grad_v[:, 4 * h:4 * h + 4, W * g:W * (g + 1)])
+
+        def load_e(j):
+            e_raw[j] = keep("e_raw%d" % j, [P, 4, 256], I32)
+            nc.sync.dma_start(out=e_raw[j][:], in_=words_v[:, :, 256 * j:256 * (j + 1)])
+
+        def load_back(kh, j):
+            back_raw[kh, j] = keep("back_raw%d%d" % (kh, j), [P, 4, 2 * W], BF16)
+            for r in range(4):
+                nc.sync.dma_start(out=back_raw[kh, j][r:P:4, :, :], in_=back_v[j, r][:, :, 2 * W * kh:2 * W * (kh + 1)])
+
+        load_grad(0, 0)
+        nc.sync.dma_start(out=mu_col[:], in_=mu.rearrange("(p m) -> p m", m=8))
+        nc.sync.dma_start(out=vec_rows[0:4, :].rearrange("t (a r) -> t a r", r=4),
+                            in_=lam.rearrange("(a t r) -> t a r", t=4, r=4))
+        nc.sync.dma_start(out=vec_rows[4:8, :].rearrange("t (a r) -> t a r", r=4),
+                            in_=radius.rearrange("(a t r) -> t a r", t=4, r=4))
+        load_grad(0, 1)
+        load_e(0)
+        scale_rows = basis_scales.bitcast(I32).rearrange("g (q r) n -> r q g n", r=4)
+        for r in range(4):
+            nc.sync.dma_start(out=scale_raw[:].bitcast(I32)[r:P:32, :, :], in_=scale_rows[r])
+        load_grad(0, 2)
+        load_back(0, 0)
+        load_grad(0, 3)
+        load_e(1)
+        load_back(0, 1)
+        load_grad(1, 0)
+        load_grad(1, 1)
+
+        vec = keep("vec", [P, 2, 8], F32)
+        ln_mu = keep("ln_mu", [P, M], F32)
+        ln_lam = keep("ln_lam", [P, 2, 4], F32)
+        inv_lam = keep("inv_lam", [P, 2, 4], F32)
+        neg_rad = keep("neg_rad", [P, 2, 4], F32)
+
+        def spread_mu():
+            mu_bank = bank(3, [P, 4, P], F32)
+            for w in range(4):
+                nc.tensor.transpose(mu_bank[:, w, :], mu_col[:].bitcast(F32)[:, w:w + 1].to_broadcast([P, P]), ident_f[:])
+            nc.scalar.activation(out=ln_mu[:].rearrange("p (w e r) -> p w e r", w=4, e=2),
+                                 in_=mu_bank[:].bitcast(BF16).rearrange("p w (r e) -> p w e r", e=2), func=ACT.Ln)
+
+        def spread_vectors():
+            vec_bank = bank(2, [P, 2, P], BF16)
+            for j in range(2):
+                nc.tensor.transpose(vec_bank[:, j, :], vec_rows[:, P * j:P * (j + 1)], ident_b[:])
+            nc.scalar.copy(out=vec[:], in_=vec_bank[:, :, 0:8])
+            nc.scalar.activation(out=ln_lam[:], in_=vec[:, :, 0:4], func=ACT.Ln)
+
+        def small_vectors():
+            nc.vector.reciprocal(out=inv_lam[:], in_=vec[:, :, 0:4])
+            nc.vector.tensor_scalar(out=neg_rad[:], in0=vec[:, :, 4:8], scalar1=-1.0, scalar2=None, op0=ALU.mult)
+
+        e_codes, e_scales = {}, {}
+
+        def sort_e_codes(j):
+            e_codes[j] = keep("e_codes%d" % j, [P, 4, 4, 256], U8)
+            nc.vector.tensor_copy(
+                out=e_codes[j][:].bitcast(I32).rearrange("p g t (a w) -> p g t a w", w=2),
+                in_=e_raw[j][:].rearrange("p g (a t w) -> p g t a w", t=4, w=2))
+
+        def sort_e_scales(j):
+            e_scales[j] = keep("e_scales%d" % j, [P, 4, 4, P], U8)
+            nc.vector.tensor_copy(
+                out=e_scales[j][:].bitcast(I32),
+                in_=scale_raw[:].bitcast(I32)[:, :, P * j:P * (j + 1)].rearrange("p g (a t) -> p g t a", t=4))
+
+        sig = {}
+
+        def sigmoid(h, j, t):
+            sig[h, j, t] = sb.tile([P, W], F32, name="sig", tag="sig", bufs=12, align_bytes=64)
+            nc.scalar.activation(out=sig[h, j, t][:], in_=ln_mu[:, W * h:W * (h + 1)], func=ACT.Sigmoid,
+                                 bias=ln_lam[:, j, t:t + 1], scale=-1.0)
+
+        turned, g_grouped, g_codes, g_scales = {}, {}, {}, {}
+
+        def turn(h, g, b0):
+            words = grad_raw[h, g][:].bitcast(F32)
+            for half in range(2):
+                turned[h, g, half] = bank(b0 + half, [P, 2, 2, P], F32)
+                for m in range(2):
+                    for u in range(2):
+                        nc.tensor.transpose(turned[h, g, half][:, m, u, :], words[:, 2 * half + m, u:256:2], ident_f[:])
+
+        def turn_out(h, g, on_vector, halves=(0, 1)):
+            if halves[0] == 0:
+                g_grouped[h, g] = sb.tile([P, 4 * W], BF16, name="g_grouped", tag="g_grouped", bufs=3, align_bytes=64)
+            dst = g_grouped[h, g][:].bitcast(F32).rearrange("p (s m r u) -> p s m r u", s=2, m=2, u=2)
+            for half in halves:
+                src = turned[h, g, half][:].rearrange("p m u r -> p m r u")
+                if on_vector:
+                    nc.vector.tensor_copy(out=dst[:, half], in_=src)
+                else:
+                    nc.scalar.copy(out=dst[:, half], in_=src)
+
+        def quantise(name, src, fmt):
+            codes = keep(name + "c", [P, W], U32)
+            scales = keep(name + "s", [P, W], U8)
+            nc.vector.quantize_mx(out=codes[:].bitcast(fmt), scales=scales[:], in_=src)
+            return codes, scales
+
+        def quant_grad(h, g):
+            g_codes[h, g], g_scales[h, g] = quantise("gq%d%d" % (h, g), g_grouped[h, g][:], E4M3X4)
+
+        coef = {}
+
+        def stage1(h, j, t, g, b):
+            if g == 0:
+                coef[h, j, t] = bank(b, [P, W], F32)
+            nc.tensor.matmul_mx(out=coef[h, j, t][:], lhsT=e_codes[j][:, g, t, :].bitcast(E2M1X4),
+                                lhsT_scale=e_scales[j][:, g, t, :],
+                                rhs=g_codes[h, g][:].bitcast(E4M3X4), rhs_scale=g_scales[h, g][:],
+                                start=(g == 0), stop=(g == 3))
+
+        y, z, z_grouped, z_codes, z_scales = {}, {}, {}, {}, {}
+
+        def divide(h, j, t):
+            y[h, j, t] = sb.tile([P, W], BF16, name="y", tag="y", bufs=6, align_bytes=64)
+            nc.vector.scalar_tensor_tensor(out=y[h, j, t][:], in0=coef[h, j, t][:], scalar=inv_lam[:, j, t:t + 1],
+                                           in1=sig[h, j, t][:], op0=ALU.mult, op1=ALU.mult)
+
+        def clip(h, j, t):
+            if t == 0:
+                z[h, j] = sb.tile([P, 4, W], BF16, name="z", tag="z", bufs=1, align_bytes=64)
+            nc.vector.tensor_scalar(out=z[h, j][:, t, :], in0=y[h, j, t][:], scalar1=vec[:, j, 4 + t:5 + t],
+                                    scalar2=neg_rad[:, j, t:t + 1], op0=ALU.min, op1=ALU.max)
+
+        def interleave(dst, src, on_vector):
+            d = dst.rearrange("p (c i t) -> p c t i", i=4, t=4)
+            s = src.rearrange("p t (c i) -> p c t i", i=4)
+            if on_vector:
+                nc.vector.tensor_copy(out=d, in_=s)
+            else:
+                nc.scalar.copy(out=d, in_=s)
+
+        def group_z(h, j, on_vector=True):
+            z_grouped[h, j] = sb.tile([P, 4 * W], BF16, name="z_grouped", tag="z_grouped", bufs=2, align_bytes=64)
+            interleave(z_grouped[h, j][:], z[h, j][:], on_vector)
+
+        def quant_z(h, j):
+            z_codes[h, j], z_scales[h, j] = quantise("zq%d%d" % (h, j), z_grouped[h, j][:], E5M2X4)
+
+        b_grouped, b_codes, b_scales = {}, {}, {}
+
+        def group_back(kq, j, on_vector, halves=(0, 1)):
+            if halves[0] == 0:
+                b_grouped[kq, j] = sb.tile([P, 4 * W], BF16, name="b_grouped", tag="b_grouped", bufs=5, align_bytes=64)
+            c0, c1 = W // 2 * halves[0], W // 2 * (halves[-1] + 1)
+            interleave(b_grouped[kq, j][:, 4 * c0:4 * c1],
+                       back_raw[kq // 2, j][:, :, W * (kq % 2) + c0:W * (kq % 2) + c1], on_vector)
+
+        def quant_back(kq, j):
+            b_codes[kq, j], b_scales[kq, j] = quantise("bq%d%d" % (kq, j), b_grouped[kq, j][:], E4M3X4)
+
+        prod, staged = {}, {}
+
+        def stage2(m, kq, b):
+            h, cols = m // 4, slice(P * (m % 4), P * (m % 4 + 1))
+            prod[m, kq] = bank(b, [P, W], F32)
+            for j in range(2):
+                nc.tensor.matmul_mx(out=prod[m, kq][:], lhsT=z_codes[h, j][:, cols].bitcast(E5M2X4),
+                                    lhsT_scale=z_scales[h, j][:, cols],
+                                    rhs=b_codes[kq, j][:].bitcast(E4M3X4), rhs_scale=b_scales[kq, j][:],
+                                    start=(j == 0), stop=(j == 1))
+
+        def negate(m, kq, on_vector):
+            if m % 2 == 0:
+                staged[m // 2, kq] = sb.tile([P, 2, W], F32, name="staged", tag="staged", bufs=6, align_bytes=64)
+            dst = staged[m // 2, kq][:, m % 2, :]
+            if on_vector:
+                nc.vector.tensor_scalar(out=dst, in0=prod[m, kq][:], scalar1=-1.0, scalar2=None, op0=ALU.mult)
+            else:
+                nc.scalar.activation(out=dst, in_=prod[m, kq][:], func=ACT.Copy, scale=-1.0)
+            if m % 2 == 1:
+                nc.sync.dma_start(out=out_v[:, m - 1:m + 1, W * kq:W * (kq + 1)], in_=staged[m // 2, kq][:])
+
+        def passes(h, j, g, b0):
+            for t in range(4):
+                stage1(h, j, t, g, b0 + t)
+
+        def finish_z(h, j):
+            for t in range(4):
+                clip(h, j, t)
+            group_z(h, j)
+
+        def tile_passes(h, j, t, b):
+            for g in range(4):
+                stage1(h, j, t, g, b)
+
+        def each_t(step, h, j):
+            for t in range(4):
+                step(h, j, t)
+
+        spread_mu()
+        spread_vectors()
+        turn(0, 0, 4)
+        turn(0, 1, 6)
+        load_grad(1, 2)
+        load_grad(1, 3)
+        load_back(1, 0)
+        load_back(1, 1)
+        turn_out(0, 0, True, (0,))
+        sort_e_codes(0)
+        turn_out(0, 0, True, (1,))
+        sort_e_scales(0)
+        quant_grad(0, 0)
+        turn_out(0, 1, True)
+        passes(0, 0, 0, 0)
+        sort_e_scales(1)
+        quant_grad(0, 1)
+        small_vectors()
+        group_back(0, 0, True)
+        group_back(1, 0, True)
+        each_t(sigmoid, 0, 0)
+        turn(0, 2, 4)
+        turn_out(0, 2, False)
+        passes(0, 0, 1, 0)
+        quant_grad(0, 2)
+        sort_e_codes(1)
+        quant_back(0, 0)
+        sigmoid(0, 1, 0)
+        sigmoid(0, 1, 1)
+        turn(0, 3, 6)
+        turn_out(0, 3, False)
+        passes(0, 0, 2, 0)
+        quant_grad(0, 3)
+        quant_back(1, 0)
+        group_back(0, 1, True)
+        for g in range(2):
+            stage1(0, 1, 0, g, 4)
+            stage1(0, 1, 1, g, 5)
+        passes(0, 0, 3, 0)
+        sigmoid(0, 1, 2)
+        sigmoid(0, 1, 3)
+        group_back(1, 1, False)
+        sigmoid(1, 0, 0)
+        sigmoid(1, 0, 1)
+        each_t(divide, 0, 0)
+        for t in range(2):
+            for g in range(2, 4):
+                stage1(0, 1, t, g, 4 + t)
+        turn(1, 0, 0)
+        turn_out(1, 0, False)
+        sigmoid(1, 0, 2)
+        sigmoid(1, 0, 3)
+        divide(0, 1, 0)
+        divide(0, 1, 1)
+        quant_grad(1, 0)
+        tile_passes(0, 1, 2, 6)
+        each_t(clip, 0, 0)
+        divide(0, 1, 2)
+        group_z(0, 0)
+        turn(1, 1, 2)
+        turn_out(1, 1, False)
+        sigmoid(1, 1, 0)
+        sigmoid(1, 1, 1)
+        tile_passes(0, 1, 3, 7)
+        divide(0, 1, 3)
+        quant_grad(1, 1)
+        quant_z(0, 0)
+        each_t(clip, 0, 1)
+        turn(1, 2, 0)
+        turn_out(1, 2, False)
+        sigmoid(1, 1, 2)
+        sigmoid(1, 1, 3)
+        quant_grad(1, 2)
+        quant_back(0, 1)
+        passes(1, 0, 0, 4)
+        turn(1, 3, 2)
+        turn_out(1, 3, False)
+        group_back(2, 0, False)
+        group_back(2, 1, False)
+        quant_grad(1, 3)
+        group_z(0, 1)
+        quant_back(1, 1)
+        quant_z(0, 1)
+        passes(1, 0, 1, 4)
+        passes(1, 0, 2, 4)
+        passes(1, 0, 3, 4)
+        each_t(divide, 1, 0)
+        tile_passes(1, 1, 0, 0)
+        tile_passes(1, 1, 1, 1)
+        for m in range(4):
+            stage2(m, 0, 4 + m)
+            negate(m, 0, False)
+        tile_passes(1, 1, 2, 2)
+        tile_passes(1, 1, 3, 3)
+        each_t(clip, 1, 0)
+        divide(1, 1, 0)
+        group_z(1, 0, False)
+        divide(1, 1, 1)
+        divide(1, 1, 2)
+        quant_back(2, 0)
+        divide(1, 1, 3)
+        quant_back(2, 1)
+        each_t(clip, 1, 1)
+        group_z(1, 1)
+        quant_z(1, 0)
+        for kq in range(1, 3):
+            for m in range(4):
+                stage2(m, kq, 4 * (kq % 2) + m)
+                negate(m, kq, False)
+        quant_z(1, 1)
+        group_back(3, 0, True)
+        group_back(3, 1, True)
+        quant_back(3, 0)
+        quant_back(3, 1)
+        n = 4
+        for h, kq in ((1, 0), (1, 1), (1, 2), (0, 3), (1, 3)):
+            for m in range(4 * h, 4 * h + 4):
+                stage2(m, kq, n % 8)
+                negate(m, kq, n >= 8 and m % 2 == 1)
+                n = n + 1

@@ -34,15 +34,16 @@ def tile_trust_region_step_s9_kernel(tc, grad, basis_words, basis_scales, lam, m
         def bank(b, shape, dtype):
             return ps.tile(shape, dtype, name="bank%d" % b, tag="bank%d" % b)
 
-        vec_rows = keep("vec_rows", [P, 2 * P], BF16)
+        lam_raw = keep("lam_raw", [P, 2, 16], BF16)
+        rad_raw = keep("rad_raw", [P, 2, 16], BF16)
         scale_raw = keep("scale_raw", [P, 4, N], U8)
         mu_col = keep("mu_col", [P, 8], BF16)
-        ident_b = keep("ident_b", [P, P], BF16)
         ident_f = keep("ident_f", [P, P], F32)
-        nc.vector.memset(vec_rows[:], 0.0)
         nc.vector.memset(scale_raw[:].bitcast(I32), 0)
         make_identity(nc, ident_f[:])
-        nc.vector.tensor_copy(out=ident_b[:], in_=ident_f[:])
+        for r in range(4):
+            nc.gpsimd.dma_start(out=rad_raw[r:P:4, :, 0:13],
+                                in_=radius.rearrange("(j a c) -> a j c", j=2, c=16)[:, :, r:r + 13])
 
         grad_v = grad.rearrange("(p m) k -> p m k", m=8)
         out_v = out.rearrange("(p m) k -> p m k", m=8)
@@ -54,9 +55,9 @@ def tile_trust_region_step_s9_kernel(tc, grad, basis_words, basis_scales, lam, m
             grad_raw[h, g] = sb.tile([P, 4, W], BF16, name="grad_raw", tag="grad_raw", bufs=6, align_bytes=64)
             nc.sync.dma_start(out=grad_raw[h, g][:], in_=grad_v[:, 4 * h:4 * h + 4, W * g:W * (g + 1)])
 
-        def load_e(j):
-            e_raw[j] = keep("e_raw%d" % j, [P, 4, 256], I32)
-            nc.sync.dma_start(out=e_raw[j][:], in_=words_v[:, :, 256 * j:256 * (j + 1)])
+        def load_e(gp):
+            e_raw[gp] = keep("e_raw%d" % gp, [P, 2, W], I32)
+            nc.sync.dma_start(out=e_raw[gp][:], in_=words_v[:, 2 * gp:2 * gp + 2, :])
 
         def load_back(kh, j):
             back_raw[kh, j] = keep("back_raw%d%d" % (kh, j), [P, 4, 2 * W], BF16)
@@ -65,24 +66,23 @@ def tile_trust_region_step_s9_kernel(tc, grad, basis_words, basis_scales, lam, m
 
         load_grad(0, 0)
         nc.sync.dma_start(out=mu_col[:], in_=mu.rearrange("(p m) -> p m", m=8))
-        nc.sync.dma_start(out=vec_rows[0:4, :].rearrange("t (a r) -> t a r", r=4),
-                            in_=lam.rearrange("(a t r) -> t a r", t=4, r=4))
-        nc.sync.dma_start(out=vec_rows[4:8, :].rearrange("t (a r) -> t a r", r=4),
-                            in_=radius.rearrange("(a t r) -> t a r", t=4, r=4))
-        load_grad(0, 1)
-        load_e(0)
         scale_rows = basis_scales.bitcast(I32).rearrange("g (q r) n -> r q g n", r=4)
         for r in range(4):
             nc.sync.dma_start(out=scale_raw[:].bitcast(I32)[r:P:32, :, :], in_=scale_rows[r])
+        load_grad(0, 1)
+        load_e(0)
+        for r in range(4):
+            nc.sync.dma_start(out=lam_raw[r:P:4, :, 0:13],
+                              in_=lam.rearrange("(j a c) -> a j c", j=2, c=16)[:, :, r:r + 13])
         load_grad(0, 2)
         load_back(0, 0)
-        load_grad(0, 3)
         load_e(1)
+        load_grad(0, 3)
         load_back(0, 1)
         load_grad(1, 0)
         load_grad(1, 1)
 
-        vec = keep("vec", [P, 2, 8], F32)
+        rad = keep("rad", [P, 2, 4], F32)
         ln_mu = keep("ln_mu", [P, M], F32)
         ln_lam = keep("ln_lam", [P, 2, 4], F32)
         inv_lam = keep("inv_lam", [P, 2, 4], F32)
@@ -95,24 +95,21 @@ def tile_trust_region_step_s9_kernel(tc, grad, basis_words, basis_scales, lam, m
             nc.scalar.activation(out=ln_mu[:].rearrange("p (w e r) -> p w e r", w=4, e=2),
                                  in_=mu_bank[:].bitcast(BF16).rearrange("p w (r e) -> p w e r", e=2), func=ACT.Ln)
 
-        def spread_vectors():
-            vec_bank = bank(2, [P, 2, P], BF16)
-            for j in range(2):
-                nc.tensor.transpose(vec_bank[:, j, :], vec_rows[:, P * j:P * (j + 1)], ident_b[:])
-            nc.scalar.copy(out=vec[:], in_=vec_bank[:, :, 0:8])
-            nc.scalar.activation(out=ln_lam[:], in_=vec[:, :, 0:4], func=ACT.Ln)
+        def log_lam():
+            nc.scalar.activation(out=ln_lam[:], in_=lam_raw[:, :, 0:13:4], func=ACT.Ln)
 
         def small_vectors():
-            nc.vector.reciprocal(out=inv_lam[:], in_=vec[:, :, 0:4])
-            nc.vector.tensor_scalar(out=neg_rad[:], in0=vec[:, :, 4:8], scalar1=-1.0, scalar2=None, op0=ALU.mult)
+            nc.vector.reciprocal(out=inv_lam[:], in_=lam_raw[:, :, 0:13:4])
+            nc.vector.tensor_copy(out=rad[:], in_=rad_raw[:, :, 0:13:4])
+            nc.vector.tensor_scalar(out=neg_rad[:], in0=rad_raw[:, :, 0:13:4], scalar1=-1.0, scalar2=None, op0=ALU.mult)
 
         e_codes, e_scales = {}, {}
 
-        def sort_e_codes(j):
-            e_codes[j] = keep("e_codes%d" % j, [P, 4, 4, 256], U8)
+        def sort_e_codes(j, gp):
+            e_codes[j, gp] = keep("e_codes%d%d" % (j, gp), [P, 2, 4, 256], U8)
             nc.vector.tensor_copy(
-                out=e_codes[j][:].bitcast(I32).rearrange("p g t (a w) -> p g t a w", w=2),
-                in_=e_raw[j][:].rearrange("p g (a t w) -> p g t a w", t=4, w=2))
+                out=e_codes[j, gp][:].bitcast(I32).rearrange("p g t (a w) -> p g t a w", w=2),
+                in_=e_raw[gp][:, :, 256 * j:256 * (j + 1)].rearrange("p g (a t w) -> p g t a w", t=4, w=2))
 
         def sort_e_scales(j):
             e_scales[j] = keep("e_scales%d" % j, [P, 4, 4, P], U8)
@@ -162,7 +159,7 @@ def tile_trust_region_step_s9_kernel(tc, grad, basis_words, basis_scales, lam, m
         def stage1(h, j, t, g, b):
             if g == 0:
                 coef[h, j, t] = bank(b, [P, W], F32)
-            nc.tensor.matmul_mx(out=coef[h, j, t][:], lhsT=e_codes[j][:, g, t, :].bitcast(E2M1X4),
+            nc.tensor.matmul_mx(out=coef[h, j, t][:], lhsT=e_codes[j, g // 2][:, g % 2, t, :].bitcast(E2M1X4),
                                 lhsT_scale=e_scales[j][:, g, t, :],
                                 rhs=g_codes[h, g][:].bitcast(E4M3X4), rhs_scale=g_scales[h, g][:],
                                 start=(g == 0), stop=(g == 3))
@@ -177,7 +174,7 @@ def tile_trust_region_step_s9_kernel(tc, grad, basis_words, basis_scales, lam, m
         def clip(h, j, t):
             if t == 0:
                 z[h, j] = sb.tile([P, 4, W], BF16, name="z", tag="z", bufs=1, align_bytes=64)
-            nc.vector.tensor_scalar(out=z[h, j][:, t, :], in0=y[h, j, t][:], scalar1=vec[:, j, 4 + t:5 + t],
+            nc.vector.tensor_scalar(out=z[h, j][:, t, :], in0=y[h, j, t][:], scalar1=rad[:, j, t:t + 1],
                                     scalar2=neg_rad[:, j, t:t + 1], op0=ALU.min, op1=ALU.max)
 
         def interleave(dst, src, on_vector):
@@ -218,16 +215,20 @@ def tile_trust_region_step_s9_kernel(tc, grad, basis_words, basis_scales, lam, m
                                     rhs=b_codes[kq, j][:].bitcast(E4M3X4), rhs_scale=b_scales[kq, j][:],
                                     start=(j == 0), stop=(j == 1))
 
-        def negate(m, kq, on_vector):
-            if m % 2 == 0:
-                staged[m // 2, kq] = sb.tile([P, 2, W], F32, name="staged", tag="staged", bufs=6, align_bytes=64)
-            dst = staged[m // 2, kq][:, m % 2, :]
+        def negate(m, kq, on_vector, pair_rows):
+            slot = m % 2 if pair_rows else kq % 2
+            key = (m // 2, kq, 0) if pair_rows else (m, kq // 2, 1)
+            if slot == 0:
+                staged[key] = sb.tile([P, 2, W], F32, name="staged", tag="staged", bufs=6, align_bytes=64)
+            dst = staged[key][:, slot, :]
             if on_vector:
                 nc.vector.tensor_scalar(out=dst, in0=prod[m, kq][:], scalar1=-1.0, scalar2=None, op0=ALU.mult)
             else:
                 nc.scalar.activation(out=dst, in_=prod[m, kq][:], func=ACT.Copy, scale=-1.0)
-            if m % 2 == 1:
-                nc.sync.dma_start(out=out_v[:, m - 1:m + 1, W * kq:W * (kq + 1)], in_=staged[m // 2, kq][:])
+            if slot == 1 and pair_rows:
+                nc.sync.dma_start(out=out_v[:, m - 1:m + 1, W * kq:W * (kq + 1)], in_=staged[key][:])
+            elif slot == 1:
+                nc.sync.dma_start(out=out_v[:, m, W * (kq - 1):W * (kq + 1)], in_=staged[key][:].rearrange("p s w -> p (s w)"))
 
         def passes(h, j, g, b0):
             for t in range(4):
@@ -247,53 +248,53 @@ def tile_trust_region_step_s9_kernel(tc, grad, basis_words, basis_scales, lam, m
                 step(h, j, t)
 
         spread_mu()
-        spread_vectors()
+        log_lam()
+        sort_e_scales(0)
+        sort_e_scales(1)
         turn(0, 0, 4)
         turn(0, 1, 6)
         load_grad(1, 2)
         load_grad(1, 3)
         load_back(1, 0)
         load_back(1, 1)
-        turn_out(0, 0, True, (0,))
-        sort_e_codes(0)
-        turn_out(0, 0, True, (1,))
-        sort_e_scales(0)
+        turn_out(0, 0, True)
+        sort_e_codes(0, 0)
         quant_grad(0, 0)
-        turn_out(0, 1, True)
+        turn_out(0, 1, True, (0,))
+        sort_e_codes(1, 0)
+        turn_out(0, 1, True, (1,))
         passes(0, 0, 0, 0)
-        sort_e_scales(1)
-        quant_grad(0, 1)
         small_vectors()
+        quant_grad(0, 1)
         group_back(0, 0, True)
         group_back(1, 0, True)
         each_t(sigmoid, 0, 0)
         turn(0, 2, 4)
         turn_out(0, 2, False)
         passes(0, 0, 1, 0)
+        sort_e_codes(0, 1)
         quant_grad(0, 2)
-        sort_e_codes(1)
+        sort_e_codes(1, 1)
         quant_back(0, 0)
-        sigmoid(0, 1, 0)
-        sigmoid(0, 1, 1)
+        each_t(sigmoid, 0, 1)
+        for g in range(2):
+            for t in range(2):
+                stage1(0, 1, t, g, 4 + t)
         turn(0, 3, 6)
         turn_out(0, 3, False)
         passes(0, 0, 2, 0)
-        quant_grad(0, 3)
         quant_back(1, 0)
+        quant_grad(0, 3)
         group_back(0, 1, True)
-        for g in range(2):
-            stage1(0, 1, 0, g, 4)
-            stage1(0, 1, 1, g, 5)
+        for t in range(2):
+            stage1(0, 1, t, 2, 4 + t)
         passes(0, 0, 3, 0)
-        sigmoid(0, 1, 2)
-        sigmoid(0, 1, 3)
         group_back(1, 1, False)
         sigmoid(1, 0, 0)
         sigmoid(1, 0, 1)
         each_t(divide, 0, 0)
         for t in range(2):
-            for g in range(2, 4):
-                stage1(0, 1, t, g, 4 + t)
+            stage1(0, 1, t, 3, 4 + t)
         turn(1, 0, 0)
         turn_out(1, 0, False)
         sigmoid(1, 0, 2)
@@ -335,9 +336,10 @@ def tile_trust_region_step_s9_kernel(tc, grad, basis_words, basis_scales, lam, m
         each_t(divide, 1, 0)
         tile_passes(1, 1, 0, 0)
         tile_passes(1, 1, 1, 1)
-        for m in range(4):
-            stage2(m, 0, 4 + m)
-            negate(m, 0, False)
+        for m in range(2):
+            for kq in range(2):
+                stage2(m, kq, 4 + 2 * m + kq)
+                negate(m, kq, False, False)
         tile_passes(1, 1, 2, 2)
         tile_passes(1, 1, 3, 3)
         each_t(clip, 1, 0)
@@ -351,18 +353,22 @@ def tile_trust_region_step_s9_kernel(tc, grad, basis_words, basis_scales, lam, m
         each_t(clip, 1, 1)
         group_z(1, 1)
         quant_z(1, 0)
-        for kq in range(1, 3):
-            for m in range(4):
-                stage2(m, kq, 4 * (kq % 2) + m)
-                negate(m, kq, False)
+        for m in range(2, 4):
+            for kq in range(2):
+                stage2(m, kq, 2 * m + kq)
+                negate(m, kq, False, False)
+        for m in range(4):
+            stage2(m, 2, m)
+            negate(m, 2, False, True)
         quant_z(1, 1)
         group_back(3, 0, True)
         group_back(3, 1, True)
         quant_back(3, 0)
         quant_back(3, 1)
         n = 4
-        for h, kq in ((1, 0), (1, 1), (1, 2), (0, 3), (1, 3)):
-            for m in range(4 * h, 4 * h + 4):
-                stage2(m, kq, n % 8)
-                negate(m, kq, n >= 8 and m % 2 == 1)
-                n = n + 1
+        rest = ([(m, kq, False) for m in range(4, 8) for kq in range(2)] + [(m, 3, True) for m in range(4)]
+                + [(m, kq, False) for m in range(4, 8) for kq in range(2, 4)])
+        for m, kq, pair_rows in rest:
+            stage2(m, kq, n % 8)
+            negate(m, kq, n >= 8 and n % 2 == 1, pair_rows)
+            n = n + 1

@@ -19,6 +19,18 @@ ALU = mybir.AluOpType
 
 P = 128
 W = 512
+SLOTS = 4
+TILES = 4
+RUN = 13
+LOW, HIGH, BANKS = 0, 4, 8
+
+GRAD_BUFS = 6
+SIG_BUFS = 12
+TURNED_BUFS = 3
+QUOTIENT_BUFS = 6
+Z_WORD_BUFS = 2
+BACK_WORD_BUFS = 5
+STAGED_BUFS = 6
 
 
 def tile_trust_region_step_s9_kernel(tc, grad, basis_words, basis_scales, lam, mu, radius, back, out):
@@ -27,348 +39,305 @@ def tile_trust_region_step_s9_kernel(tc, grad, basis_words, basis_scales, lam, m
         sb = ctx.enter_context(tc.tile_pool(name="sb", bufs=1))
         ps = ctx.enter_context(tc.psum_pool(name="ps", bufs=1))
         ctx.enter_context(tc.manual_schedule())
+        on_vector, on_scalar = nc.vector.tensor_copy, nc.scalar.copy
 
-        def keep(name, shape, dtype):
-            return sb.tile(shape, dtype, name=name, tag=name, align_bytes=64)
+        def sbuf(name, shape, dtype, bufs=1):
+            return sb.tile(shape, dtype, name=name, tag=name, bufs=bufs, align_bytes=64)
 
-        def bank(b, shape, dtype):
-            return ps.tile(shape, dtype, name="bank%d" % b, tag="bank%d" % b)
+        def bank(b, shape):
+            return ps.tile(shape, F32, name="bank%d" % b, tag="bank%d" % b)
 
-        lam_raw = keep("lam_raw", [P, 2, 16], BF16)
-        rad_raw = keep("rad_raw", [P, 2, 16], BF16)
-        scale_raw = keep("scale_raw", [P, 4, N], U8)
-        mu_col = keep("mu_col", [P, 8], BF16)
-        ident_f = keep("ident_f", [P, P], F32)
-        nc.vector.memset(scale_raw[:].bitcast(I32), 0)
-        make_identity(nc, ident_f[:])
-        for r in range(4):
-            nc.gpsimd.dma_start(out=rad_raw[r:P:4, :, 0:13],
-                                in_=radius.rearrange("(j a c) -> a j c", j=2, c=16)[:, :, r:r + 13])
-
-        grad_v = grad.rearrange("(p m) k -> p m k", m=8)
-        out_v = out.rearrange("(p m) k -> p m k", m=8)
-        words_v = basis_words.bitcast(I32).rearrange("g p w -> p g w")
-        back_v = back.rearrange("(g a t r) k -> g r a t k", g=2, t=4, r=4)
+        lam_raw = sbuf("lam_raw", [P, 2, 16], BF16)
+        rad_raw = sbuf("rad_raw", [P, 2, 16], BF16)
+        scale_raw = sbuf("scale_raw", [P, 4, N], U8)
+        mu_col = sbuf("mu_col", [P, 2 * TILES], BF16)
+        identity = sbuf("identity", [P, P], F32)
+        grad_rows = grad.rearrange("(p m) k -> p m k", m=2 * TILES)
+        out_rows = out.rearrange("(p m) k -> p m k", m=2 * TILES)
+        e_words = basis_words.bitcast(I32).rearrange("g p w -> p g w")
+        back_rows = back.rearrange("(s a t r) k -> s r a t k", s=2, t=SLOTS, r=4)
         grad_raw, e_raw, back_raw = {}, {}, {}
 
         def load_grad(h, g):
-            grad_raw[h, g] = sb.tile([P, 4, W], BF16, name="grad_raw", tag="grad_raw", bufs=6, align_bytes=64)
-            nc.sync.dma_start(out=grad_raw[h, g][:], in_=grad_v[:, 4 * h:4 * h + 4, W * g:W * (g + 1)])
+            grad_raw[h, g] = sbuf("grad_raw", [P, TILES, W], BF16, GRAD_BUFS)
+            nc.sync.dma_start(out=grad_raw[h, g][:], in_=grad_rows[:, TILES * h:TILES * (h + 1), W * g:W * (g + 1)])
 
-        def load_e(gp):
-            e_raw[gp] = keep("e_raw%d" % gp, [P, 2, W], I32)
-            nc.sync.dma_start(out=e_raw[gp][:], in_=words_v[:, 2 * gp:2 * gp + 2, :])
+        def load_e_codes(gp):
+            e_raw[gp] = sbuf("e_raw%d" % gp, [P, 2, N // 2], I32)
+            nc.sync.dma_start(out=e_raw[gp][:], in_=e_words[:, 2 * gp:2 * gp + 2, :])
 
-        def load_back(kh, j):
-            back_raw[kh, j] = keep("back_raw%d%d" % (kh, j), [P, 4, 2 * W], BF16)
+        def load_e_scales():
+            rows = basis_scales.bitcast(I32).rearrange("g (q r) n -> r q g n", r=4)
             for r in range(4):
-                nc.sync.dma_start(out=back_raw[kh, j][r:P:4, :, :], in_=back_v[j, r][:, :, 2 * W * kh:2 * W * (kh + 1)])
+                nc.sync.dma_start(out=scale_raw[:].bitcast(I32)[r:P:32, :, :], in_=rows[r])
+
+        def load_by_direction(tile, vector):
+            for r in range(4):
+                nc.sync.dma_start(out=tile[r:P:4, :, 0:RUN],
+                                  in_=vector.rearrange("(s a c) -> a s c", s=2, c=16)[:, :, r:r + RUN])
+
+        def load_back(kh, s):
+            back_raw[kh, s] = sbuf("back_raw%d%d" % (kh, s), [P, SLOTS, 2 * W], BF16)
+            for r in range(4):
+                nc.sync.dma_start(out=back_raw[kh, s][r:P:4, :, :],
+                                  in_=back_rows[s, r][:, :, 2 * W * kh:2 * W * (kh + 1)])
+
+        nc.vector.memset(scale_raw[:].bitcast(I32), 0)
+        make_identity(nc, identity[:])
 
         load_grad(0, 0)
-        nc.sync.dma_start(out=mu_col[:], in_=mu.rearrange("(p m) -> p m", m=8))
-        scale_rows = basis_scales.bitcast(I32).rearrange("g (q r) n -> r q g n", r=4)
-        for r in range(4):
-            nc.sync.dma_start(out=scale_raw[:].bitcast(I32)[r:P:32, :, :], in_=scale_rows[r])
+        nc.sync.dma_start(out=mu_col[:], in_=mu.rearrange("(p m) -> p m", m=2 * TILES))
+        load_e_scales()
         load_grad(0, 1)
-        load_e(0)
-        for r in range(4):
-            nc.sync.dma_start(out=lam_raw[r:P:4, :, 0:13],
-                              in_=lam.rearrange("(j a c) -> a j c", j=2, c=16)[:, :, r:r + 13])
+        load_e_codes(0)
+        load_by_direction(lam_raw, lam)
         load_grad(0, 2)
         load_back(0, 0)
-        load_e(1)
+        load_e_codes(1)
         load_grad(0, 3)
         load_back(0, 1)
         load_grad(1, 0)
         load_grad(1, 1)
+        load_by_direction(rad_raw, radius)
 
-        rad = keep("rad", [P, 2, 4], F32)
-        ln_mu = keep("ln_mu", [P, M], F32)
-        ln_lam = keep("ln_lam", [P, 2, 4], F32)
-        inv_lam = keep("inv_lam", [P, 2, 4], F32)
-        neg_rad = keep("neg_rad", [P, 2, 4], F32)
+        rad = sbuf("rad", [P, 2, SLOTS], F32)
+        ln_mu = sbuf("ln_mu", [P, M], F32)
+        ln_lam = sbuf("ln_lam", [P, 2, SLOTS], F32)
+        inv_lam = sbuf("inv_lam", [P, 2, SLOTS], F32)
+        neg_rad = sbuf("neg_rad", [P, 2, SLOTS], F32)
 
-        def spread_mu():
-            mu_bank = bank(3, [P, 4, P], F32)
-            for w in range(4):
-                nc.tensor.transpose(mu_bank[:, w, :], mu_col[:].bitcast(F32)[:, w:w + 1].to_broadcast([P, P]), ident_f[:])
-            nc.scalar.activation(out=ln_mu[:].rearrange("p (w e r) -> p w e r", w=4, e=2),
-                                 in_=mu_bank[:].bitcast(BF16).rearrange("p w (r e) -> p w e r", e=2), func=ACT.Ln)
+        def logarithms():
+            spread = bank(LOW + SLOTS - 1, [P, TILES, P])
+            for w in range(TILES):
+                nc.tensor.transpose(spread[:, w, :], mu_col[:].bitcast(F32)[:, w:w + 1].to_broadcast([P, P]), identity[:])
+            nc.scalar.activation(out=ln_mu[:].rearrange("q (w e p) -> q w e p", w=TILES, e=2),
+                                 in_=spread[:].bitcast(BF16).rearrange("q w (p e) -> q w e p", e=2), func=ACT.Ln)
+            nc.scalar.activation(out=ln_lam[:], in_=lam_raw[:, :, 0:RUN:4], func=ACT.Ln)
 
-        def log_lam():
-            nc.scalar.activation(out=ln_lam[:], in_=lam_raw[:, :, 0:13:4], func=ACT.Ln)
+        def invert_lam():
+            nc.vector.reciprocal(out=inv_lam[:], in_=lam_raw[:, :, 0:RUN:4])
 
-        def small_vectors():
-            nc.vector.reciprocal(out=inv_lam[:], in_=lam_raw[:, :, 0:13:4])
-            nc.vector.tensor_copy(out=rad[:], in_=rad_raw[:, :, 0:13:4])
-            nc.vector.tensor_scalar(out=neg_rad[:], in0=rad_raw[:, :, 0:13:4], scalar1=-1.0, scalar2=None, op0=ALU.mult)
+        def clip_bounds():
+            nc.vector.tensor_copy(out=rad[:], in_=rad_raw[:, :, 0:RUN:4])
+            nc.vector.tensor_scalar(out=neg_rad[:], in0=rad_raw[:, :, 0:RUN:4], scalar1=-1.0, scalar2=None, op0=ALU.mult)
 
-        e_codes, e_scales = {}, {}
+        e_codes, e_scales, turned, grad_words, grad_mx, coef = {}, {}, {}, {}, {}, {}
 
-        def sort_e_codes(j, gp):
-            e_codes[j, gp] = keep("e_codes%d%d" % (j, gp), [P, 2, 4, 256], U8)
+        def sort_e_codes(s, gp):
+            e_codes[s, gp] = sbuf("e_codes%d%d" % (s, gp), [P, 2, SLOTS, 2 * P], U8)
             nc.vector.tensor_copy(
-                out=e_codes[j, gp][:].bitcast(I32).rearrange("p g t (a w) -> p g t a w", w=2),
-                in_=e_raw[gp][:, :, 256 * j:256 * (j + 1)].rearrange("p g (a t w) -> p g t a w", t=4, w=2))
+                out=e_codes[s, gp][:].bitcast(I32).rearrange("p g t (a w) -> p g t a w", w=2),
+                in_=e_raw[gp][:, :, W // 2 * s:W // 2 * (s + 1)].rearrange("p g (a t w) -> p g t a w", t=SLOTS, w=2))
 
-        def sort_e_scales(j):
-            e_scales[j] = keep("e_scales%d" % j, [P, 4, 4, P], U8)
+        def sort_e_scales(s):
+            e_scales[s] = sbuf("e_scales%d" % s, [P, 4, SLOTS, P], U8)
             nc.vector.tensor_copy(
-                out=e_scales[j][:].bitcast(I32),
-                in_=scale_raw[:].bitcast(I32)[:, :, P * j:P * (j + 1)].rearrange("p g (a t) -> p g t a", t=4))
+                out=e_scales[s][:].bitcast(I32),
+                in_=scale_raw[:].bitcast(I32)[:, :, W // 4 * s:W // 4 * (s + 1)].rearrange("p g (a t) -> p g t a", t=SLOTS))
 
-        sig = {}
-
-        def sigmoid(h, j, t):
-            sig[h, j, t] = sb.tile([P, W], F32, name="sig", tag="sig", bufs=12, align_bytes=64)
-            nc.scalar.activation(out=sig[h, j, t][:], in_=ln_mu[:, W * h:W * (h + 1)], func=ACT.Sigmoid,
-                                 bias=ln_lam[:, j, t:t + 1], scale=-1.0)
-
-        turned, g_grouped, g_codes, g_scales = {}, {}, {}, {}
-
-        def turn(h, g, b0):
-            words = grad_raw[h, g][:].bitcast(F32)
-            for half in range(2):
-                turned[h, g, half] = bank(b0 + half, [P, 2, 2, P], F32)
+        def turn(h, g, first_bank):
+            pairs = grad_raw[h, g][:].bitcast(F32)
+            for b in range(2):
+                turned[h, g, b] = bank(first_bank + b, [P, 2, 2, P])
                 for m in range(2):
                     for u in range(2):
-                        nc.tensor.transpose(turned[h, g, half][:, m, u, :], words[:, 2 * half + m, u:256:2], ident_f[:])
+                        nc.tensor.transpose(turned[h, g, b][:, m, u, :], pairs[:, 2 * b + m, u:W // 2:2], identity[:])
 
-        def turn_out(h, g, on_vector, halves=(0, 1)):
-            if halves[0] == 0:
-                g_grouped[h, g] = sb.tile([P, 4 * W], BF16, name="g_grouped", tag="g_grouped", bufs=3, align_bytes=64)
-            dst = g_grouped[h, g][:].bitcast(F32).rearrange("p (s m r u) -> p s m r u", s=2, m=2, u=2)
-            for half in halves:
-                src = turned[h, g, half][:].rearrange("p m u r -> p m r u")
-                if on_vector:
-                    nc.vector.tensor_copy(out=dst[:, half], in_=src)
-                else:
-                    nc.scalar.copy(out=dst[:, half], in_=src)
+        def turn_out(h, g, copy, banks=(0, 1)):
+            if banks[0] == 0:
+                grad_words[h, g] = sbuf("grad_words", [P, SLOTS * W], BF16, TURNED_BUFS)
+            dst = grad_words[h, g][:].bitcast(F32).rearrange("p (b m r u) -> p b m r u", b=2, m=2, u=2)
+            for b in banks:
+                copy(out=dst[:, b], in_=turned[h, g, b][:].rearrange("p m u r -> p m r u"))
 
-        def quantise(name, src, fmt):
-            codes = keep(name + "c", [P, W], U32)
-            scales = keep(name + "s", [P, W], U8)
-            nc.vector.quantize_mx(out=codes[:].bitcast(fmt), scales=scales[:], in_=src)
+        def quantise(name, words, fmt):
+            codes = sbuf(name + "_codes", [P, W], U32)
+            scales = sbuf(name + "_scales", [P, W], U8)
+            nc.vector.quantize_mx(out=codes[:].bitcast(fmt), scales=scales[:], in_=words[:])
             return codes, scales
 
-        def quant_grad(h, g):
-            g_codes[h, g], g_scales[h, g] = quantise("gq%d%d" % (h, g), g_grouped[h, g][:], E4M3X4)
+        def quantise_grad(h, g):
+            grad_mx[h, g] = quantise("grad%d%d" % (h, g), grad_words[h, g], E4M3X4)
 
-        coef = {}
+        def coef_passes(h, s, slots, groups, first_bank):
+            for g in groups:
+                for t in slots:
+                    if g == 0:
+                        coef[h, s, t] = bank(first_bank + t, [P, W])
+                    codes, scales = grad_mx[h, g]
+                    nc.tensor.matmul_mx(out=coef[h, s, t][:], lhsT=e_codes[s, g // 2][:, g % 2, t, :].bitcast(E2M1X4),
+                                        lhsT_scale=e_scales[s][:, g, t, :], rhs=codes[:].bitcast(E4M3X4),
+                                        rhs_scale=scales[:], start=(g == 0), stop=(g == 3))
 
-        def stage1(h, j, t, g, b):
-            if g == 0:
-                coef[h, j, t] = bank(b, [P, W], F32)
-            nc.tensor.matmul_mx(out=coef[h, j, t][:], lhsT=e_codes[j, g // 2][:, g % 2, t, :].bitcast(E2M1X4),
-                                lhsT_scale=e_scales[j][:, g, t, :],
-                                rhs=g_codes[h, g][:].bitcast(E4M3X4), rhs_scale=g_scales[h, g][:],
-                                start=(g == 0), stop=(g == 3))
+        sig, quotient, z, z_words, z_mx, back_words, back_mx = {}, {}, {}, {}, {}, {}, {}
 
-        y, z, z_grouped, z_codes, z_scales = {}, {}, {}, {}, {}
+        def sigmoids(h, s, slots):
+            for t in slots:
+                sig[h, s, t] = sbuf("sig", [P, W], F32, SIG_BUFS)
+                nc.scalar.activation(out=sig[h, s, t][:], in_=ln_mu[:, W * h:W * (h + 1)], func=ACT.Sigmoid,
+                                     bias=ln_lam[:, s, t:t + 1], scale=-1.0)
 
-        def divide(h, j, t):
-            y[h, j, t] = sb.tile([P, W], BF16, name="y", tag="y", bufs=6, align_bytes=64)
-            nc.vector.scalar_tensor_tensor(out=y[h, j, t][:], in0=coef[h, j, t][:], scalar=inv_lam[:, j, t:t + 1],
-                                           in1=sig[h, j, t][:], op0=ALU.mult, op1=ALU.mult)
+        def divide(h, s, slots):
+            for t in slots:
+                quotient[h, s, t] = sbuf("quotient", [P, W], BF16, QUOTIENT_BUFS)
+                nc.vector.scalar_tensor_tensor(out=quotient[h, s, t][:], in0=coef[h, s, t][:], scalar=inv_lam[:, s, t:t + 1],
+                                               in1=sig[h, s, t][:], op0=ALU.mult, op1=ALU.mult)
 
-        def clip(h, j, t):
-            if t == 0:
-                z[h, j] = sb.tile([P, 4, W], BF16, name="z", tag="z", bufs=1, align_bytes=64)
-            nc.vector.tensor_scalar(out=z[h, j][:, t, :], in0=y[h, j, t][:], scalar1=rad[:, j, t:t + 1],
-                                    scalar2=neg_rad[:, j, t:t + 1], op0=ALU.min, op1=ALU.max)
+        def clip(h, s):
+            z[h, s] = sbuf("z", [P, SLOTS, W], BF16)
+            for t in range(SLOTS):
+                nc.vector.tensor_scalar(out=z[h, s][:, t, :], in0=quotient[h, s, t][:], scalar1=rad[:, s, t:t + 1],
+                                        scalar2=neg_rad[:, s, t:t + 1], op0=ALU.min, op1=ALU.max)
 
-        def interleave(dst, src, on_vector):
-            d = dst.rearrange("p (c i t) -> p c t i", i=4, t=4)
-            s = src.rearrange("p t (c i) -> p c t i", i=4)
-            if on_vector:
-                nc.vector.tensor_copy(out=d, in_=s)
+        def lay_words(dst, src, copy):
+            copy(out=dst.rearrange("p (c i t) -> p c t i", i=4, t=SLOTS), in_=src.rearrange("p t (c i) -> p c t i", i=4))
+
+        def lay_z(h, s, copy):
+            z_words[h, s] = sbuf("z_words", [P, SLOTS * W], BF16, Z_WORD_BUFS)
+            lay_words(z_words[h, s][:], z[h, s][:], copy)
+
+        def quantise_z(h, s):
+            z_mx[h, s] = quantise("z%d%d" % (h, s), z_words[h, s], E5M2X4)
+
+        def lay_back(kq, s, copy):
+            back_words[kq, s] = sbuf("back_words", [P, SLOTS * W], BF16, BACK_WORD_BUFS)
+            lay_words(back_words[kq, s][:], back_raw[kq // 2, s][:, :, W * (kq % 2):W * (kq % 2 + 1)], copy)
+
+        def quantise_back(kq, s):
+            back_mx[kq, s] = quantise("back%d%d" % (kq, s), back_words[kq, s], E4M3X4)
+
+        def result_pair(pair, first_bank, share):
+            staged = sbuf("staged", [P, 2, W], F32, STAGED_BUFS)
+            for n, (m, kq) in enumerate(pair):
+                cols = slice(P * (m % TILES), P * (m % TILES + 1))
+                prod = bank(first_bank + n, [P, W])
+                for s in range(2):
+                    z_codes, z_scales = z_mx[m // TILES, s]
+                    back_codes, back_scales = back_mx[kq, s]
+                    nc.tensor.matmul_mx(out=prod[:], lhsT=z_codes[:, cols].bitcast(E5M2X4), lhsT_scale=z_scales[:, cols],
+                                        rhs=back_codes[:].bitcast(E4M3X4), rhs_scale=back_scales[:],
+                                        start=(s == 0), stop=(s == 1))
+                if share and n == 1:
+                    nc.vector.tensor_scalar(out=staged[:, n, :], in0=prod[:], scalar1=-1.0, scalar2=None, op0=ALU.mult)
+                else:
+                    nc.scalar.activation(out=staged[:, n, :], in_=prod[:], func=ACT.Copy, scale=-1.0)
+            (m0, kq0), (m1, kq1) = pair
+            if m0 == m1:
+                nc.sync.dma_start(out=out_rows[:, m0, W * kq0:W * (kq1 + 1)], in_=staged[:].rearrange("p n w -> p (n w)"))
             else:
-                nc.scalar.copy(out=d, in_=s)
+                nc.sync.dma_start(out=out_rows[:, m0:m1 + 1, W * kq0:W * (kq0 + 1)], in_=staged[:])
 
-        def group_z(h, j, on_vector=True):
-            z_grouped[h, j] = sb.tile([P, 4 * W], BF16, name="z_grouped", tag="z_grouped", bufs=2, align_bytes=64)
-            interleave(z_grouped[h, j][:], z[h, j][:], on_vector)
+        def along_k(tiles, kh):
+            return [((m, 2 * kh), (m, 2 * kh + 1)) for m in tiles]
 
-        def quant_z(h, j):
-            z_codes[h, j], z_scales[h, j] = quantise("zq%d%d" % (h, j), z_grouped[h, j][:], E5M2X4)
+        def along_m(h, kq):
+            return [((m, kq), (m + 1, kq)) for m in range(TILES * h, TILES * (h + 1), 2)]
 
-        b_grouped, b_codes, b_scales = {}, {}, {}
+        every, early, late = range(4), (0, 1), (2, 3)
 
-        def group_back(kq, j, on_vector, halves=(0, 1)):
-            if halves[0] == 0:
-                b_grouped[kq, j] = sb.tile([P, 4 * W], BF16, name="b_grouped", tag="b_grouped", bufs=5, align_bytes=64)
-            c0, c1 = W // 2 * halves[0], W // 2 * (halves[-1] + 1)
-            interleave(b_grouped[kq, j][:, 4 * c0:4 * c1],
-                       back_raw[kq // 2, j][:, :, W * (kq % 2) + c0:W * (kq % 2) + c1], on_vector)
-
-        def quant_back(kq, j):
-            b_codes[kq, j], b_scales[kq, j] = quantise("bq%d%d" % (kq, j), b_grouped[kq, j][:], E4M3X4)
-
-        prod, staged = {}, {}
-
-        def stage2(m, kq, b):
-            h, cols = m // 4, slice(P * (m % 4), P * (m % 4 + 1))
-            prod[m, kq] = bank(b, [P, W], F32)
-            for j in range(2):
-                nc.tensor.matmul_mx(out=prod[m, kq][:], lhsT=z_codes[h, j][:, cols].bitcast(E5M2X4),
-                                    lhsT_scale=z_scales[h, j][:, cols],
-                                    rhs=b_codes[kq, j][:].bitcast(E4M3X4), rhs_scale=b_scales[kq, j][:],
-                                    start=(j == 0), stop=(j == 1))
-
-        def negate(m, kq, on_vector, pair_rows):
-            slot = m % 2 if pair_rows else kq % 2
-            key = (m // 2, kq, 0) if pair_rows else (m, kq // 2, 1)
-            if slot == 0:
-                staged[key] = sb.tile([P, 2, W], F32, name="staged", tag="staged", bufs=6, align_bytes=64)
-            dst = staged[key][:, slot, :]
-            if on_vector:
-                nc.vector.tensor_scalar(out=dst, in0=prod[m, kq][:], scalar1=-1.0, scalar2=None, op0=ALU.mult)
-            else:
-                nc.scalar.activation(out=dst, in_=prod[m, kq][:], func=ACT.Copy, scale=-1.0)
-            if slot == 1 and pair_rows:
-                nc.sync.dma_start(out=out_v[:, m - 1:m + 1, W * kq:W * (kq + 1)], in_=staged[key][:])
-            elif slot == 1:
-                nc.sync.dma_start(out=out_v[:, m, W * (kq - 1):W * (kq + 1)], in_=staged[key][:].rearrange("p s w -> p (s w)"))
-
-        def passes(h, j, g, b0):
-            for t in range(4):
-                stage1(h, j, t, g, b0 + t)
-
-        def finish_z(h, j):
-            for t in range(4):
-                clip(h, j, t)
-            group_z(h, j)
-
-        def tile_passes(h, j, t, b):
-            for g in range(4):
-                stage1(h, j, t, g, b)
-
-        def each_t(step, h, j):
-            for t in range(4):
-                step(h, j, t)
-
-        spread_mu()
-        log_lam()
+        logarithms()
         sort_e_scales(0)
         sort_e_scales(1)
-        turn(0, 0, 4)
-        turn(0, 1, 6)
+        turn(0, 0, HIGH)
+        turn(0, 1, HIGH + 2)
         load_grad(1, 2)
         load_grad(1, 3)
         load_back(1, 0)
         load_back(1, 1)
-        turn_out(0, 0, True)
+        turn_out(0, 0, on_vector)
         sort_e_codes(0, 0)
-        quant_grad(0, 0)
-        turn_out(0, 1, True, (0,))
+        quantise_grad(0, 0)
+        turn_out(0, 1, on_vector, (0,))
         sort_e_codes(1, 0)
-        turn_out(0, 1, True, (1,))
-        passes(0, 0, 0, 0)
-        small_vectors()
-        quant_grad(0, 1)
-        group_back(0, 0, True)
-        group_back(1, 0, True)
-        each_t(sigmoid, 0, 0)
-        turn(0, 2, 4)
-        turn_out(0, 2, False)
-        passes(0, 0, 1, 0)
+        turn_out(0, 1, on_vector, (1,))
+        coef_passes(0, 0, every, (0,), LOW)
+        invert_lam()
+        quantise_grad(0, 1)
+        lay_back(0, 0, on_vector)
+        lay_back(1, 0, on_vector)
+        sigmoids(0, 0, every)
+        turn(0, 2, HIGH)
+        turn_out(0, 2, on_scalar)
+        coef_passes(0, 0, every, (1,), LOW)
         sort_e_codes(0, 1)
-        quant_grad(0, 2)
+        quantise_grad(0, 2)
         sort_e_codes(1, 1)
-        quant_back(0, 0)
-        each_t(sigmoid, 0, 1)
-        for g in range(2):
-            for t in range(2):
-                stage1(0, 1, t, g, 4 + t)
-        turn(0, 3, 6)
-        turn_out(0, 3, False)
-        passes(0, 0, 2, 0)
-        quant_back(1, 0)
-        quant_grad(0, 3)
-        group_back(0, 1, True)
-        for t in range(2):
-            stage1(0, 1, t, 2, 4 + t)
-        passes(0, 0, 3, 0)
-        group_back(1, 1, False)
-        sigmoid(1, 0, 0)
-        sigmoid(1, 0, 1)
-        each_t(divide, 0, 0)
-        for t in range(2):
-            stage1(0, 1, t, 3, 4 + t)
-        turn(1, 0, 0)
-        turn_out(1, 0, False)
-        sigmoid(1, 0, 2)
-        sigmoid(1, 0, 3)
-        divide(0, 1, 0)
-        divide(0, 1, 1)
-        quant_grad(1, 0)
-        tile_passes(0, 1, 2, 6)
-        each_t(clip, 0, 0)
-        divide(0, 1, 2)
-        group_z(0, 0)
-        turn(1, 1, 2)
-        turn_out(1, 1, False)
-        sigmoid(1, 1, 0)
-        sigmoid(1, 1, 1)
-        tile_passes(0, 1, 3, 7)
-        divide(0, 1, 3)
-        quant_grad(1, 1)
-        quant_z(0, 0)
-        each_t(clip, 0, 1)
-        turn(1, 2, 0)
-        turn_out(1, 2, False)
-        sigmoid(1, 1, 2)
-        sigmoid(1, 1, 3)
-        quant_grad(1, 2)
-        quant_back(0, 1)
-        passes(1, 0, 0, 4)
-        turn(1, 3, 2)
-        turn_out(1, 3, False)
-        group_back(2, 0, False)
-        group_back(2, 1, False)
-        quant_grad(1, 3)
-        group_z(0, 1)
-        quant_back(1, 1)
-        quant_z(0, 1)
-        passes(1, 0, 1, 4)
-        passes(1, 0, 2, 4)
-        passes(1, 0, 3, 4)
-        each_t(divide, 1, 0)
-        tile_passes(1, 1, 0, 0)
-        tile_passes(1, 1, 1, 1)
-        for m in range(2):
-            for kq in range(2):
-                stage2(m, kq, 4 + 2 * m + kq)
-                negate(m, kq, False, False)
-        tile_passes(1, 1, 2, 2)
-        tile_passes(1, 1, 3, 3)
-        each_t(clip, 1, 0)
-        divide(1, 1, 0)
-        group_z(1, 0, False)
-        divide(1, 1, 1)
-        divide(1, 1, 2)
-        quant_back(2, 0)
-        divide(1, 1, 3)
-        quant_back(2, 1)
-        each_t(clip, 1, 1)
-        group_z(1, 1)
-        quant_z(1, 0)
-        for m in range(2, 4):
-            for kq in range(2):
-                stage2(m, kq, 2 * m + kq)
-                negate(m, kq, False, False)
-        for m in range(4):
-            stage2(m, 2, m)
-            negate(m, 2, False, True)
-        quant_z(1, 1)
-        group_back(3, 0, True)
-        group_back(3, 1, True)
-        quant_back(3, 0)
-        quant_back(3, 1)
-        n = 4
-        rest = ([(m, kq, False) for m in range(4, 8) for kq in range(2)] + [(m, 3, True) for m in range(4)]
-                + [(m, kq, False) for m in range(4, 8) for kq in range(2, 4)])
-        for m, kq, pair_rows in rest:
-            stage2(m, kq, n % 8)
-            negate(m, kq, n >= 8 and n % 2 == 1, pair_rows)
-            n = n + 1
+        quantise_back(0, 0)
+        sigmoids(0, 1, every)
+        coef_passes(0, 1, early, early, HIGH)
+        turn(0, 3, HIGH + 2)
+        turn_out(0, 3, on_scalar)
+        coef_passes(0, 0, every, (2,), LOW)
+        quantise_back(1, 0)
+        quantise_grad(0, 3)
+        lay_back(0, 1, on_vector)
+        coef_passes(0, 1, early, (2,), HIGH)
+        coef_passes(0, 0, every, (3,), LOW)
+        lay_back(1, 1, on_scalar)
+        sigmoids(1, 0, early)
+        divide(0, 0, every)
+        coef_passes(0, 1, early, (3,), HIGH)
+
+        turn(1, 0, LOW)
+        turn_out(1, 0, on_scalar)
+        sigmoids(1, 0, late)
+        divide(0, 1, early)
+        clip_bounds()
+        quantise_grad(1, 0)
+        coef_passes(0, 1, (2,), every, HIGH)
+        clip(0, 0)
+        divide(0, 1, (2,))
+        lay_z(0, 0, on_vector)
+        turn(1, 1, LOW + 2)
+        turn_out(1, 1, on_scalar)
+        sigmoids(1, 1, early)
+        coef_passes(0, 1, (3,), every, HIGH)
+        divide(0, 1, (3,))
+        quantise_grad(1, 1)
+        quantise_z(0, 0)
+        clip(0, 1)
+        turn(1, 2, LOW)
+        turn_out(1, 2, on_scalar)
+        sigmoids(1, 1, late)
+        quantise_grad(1, 2)
+        quantise_back(0, 1)
+
+        coef_passes(1, 0, every, (0,), HIGH)
+        turn(1, 3, LOW + 2)
+        turn_out(1, 3, on_scalar)
+        lay_back(2, 0, on_scalar)
+        lay_back(2, 1, on_scalar)
+        quantise_grad(1, 3)
+        lay_z(0, 1, on_vector)
+        quantise_back(1, 1)
+        quantise_z(0, 1)
+        coef_passes(1, 0, every, (1, 2, 3), HIGH)
+        divide(1, 0, every)
+
+        for t in early:
+            coef_passes(1, 1, (t,), every, LOW)
+        for n, pair in enumerate(along_k(early, 0)):
+            result_pair(pair, HIGH + 2 * n, False)
+        for t in late:
+            coef_passes(1, 1, (t,), every, LOW)
+        clip(1, 0)
+        divide(1, 1, (0,))
+        lay_z(1, 0, on_scalar)
+        divide(1, 1, (1, 2))
+        quantise_back(2, 0)
+        divide(1, 1, (3,))
+        quantise_back(2, 1)
+        clip(1, 1)
+        lay_z(1, 1, on_vector)
+        quantise_z(1, 0)
+        for n, pair in enumerate(along_k(late, 0) + along_m(0, 2)):
+            result_pair(pair, (HIGH + 2 * n) % BANKS, False)
+        quantise_z(1, 1)
+
+        lay_back(3, 0, on_vector)
+        lay_back(3, 1, on_vector)
+        quantise_back(3, 0)
+        quantise_back(3, 1)
+        second_half = range(TILES, 2 * TILES)
+        for n, pair in enumerate(along_k(second_half, 0) + along_m(0, 3) + along_k(second_half, 1)):
+            result_pair(pair, (HIGH + 2 * n) % BANKS, n >= 2)

from contextlib import ExitStack

import concourse.mybir as mybir
from concourse.masks import make_identity

M, K, N = 1024, 2048, 1024
FLOPS = 2 * M * K * N * 2

F32 = mybir.dt.float32
BF16 = mybir.dt.bfloat16
I32 = mybir.dt.int32
U32 = mybir.dt.uint32
U8 = mybir.dt.uint8
E4M3X4 = mybir.dt.float8_e4m3fn_x4
E5M2X4 = mybir.dt.float8_e5m2_x4
E2M1X4 = mybir.dt.float4_e2m1fn_x4
ACT = mybir.ActivationFunctionType
ALU = mybir.AluOpType

P = 128
W = 512
SLOTS = 4
TILES = 4
RUN = 13
LOW, HIGH, BANKS = 0, 4, 8

GRAD_BUFS = 6
SIG_BUFS = 12
TURNED_BUFS = 3
QUOTIENT_BUFS = 6
Z_WORD_BUFS = 2
BACK_WORD_BUFS = 5
STAGED_BUFS = 6


def tile_trust_region_step_s9_kernel(tc, grad, basis_words, basis_scales, lam, mu, radius, back, out):
    nc = tc.nc
    with ExitStack() as ctx:
        sb = ctx.enter_context(tc.tile_pool(name="sb", bufs=1))
        ps = ctx.enter_context(tc.psum_pool(name="ps", bufs=1))
        ctx.enter_context(tc.manual_schedule())
        on_vector, on_scalar = nc.vector.tensor_copy, nc.scalar.copy

        def sbuf(name, shape, dtype, bufs=1):
            return sb.tile(shape, dtype, name=name, tag=name, bufs=bufs, align_bytes=64)

        def bank(b, shape):
            return ps.tile(shape, F32, name="bank%d" % b, tag="bank%d" % b)

        lam_raw = sbuf("lam_raw", [P, 2, 16], BF16)
        rad_raw = sbuf("rad_raw", [P, 2, 16], BF16)
        scale_raw = sbuf("scale_raw", [P, 4, N], U8)
        mu_col = sbuf("mu_col", [P, 2 * TILES], BF16)
        identity = sbuf("identity", [P, P], F32)
        grad_rows = grad.rearrange("(p m) k -> p m k", m=2 * TILES)
        out_rows = out.rearrange("(p m) k -> p m k", m=2 * TILES)
        e_words = basis_words.bitcast(I32).rearrange("g p w -> p g w")
        back_rows = back.rearrange("(s a t r) k -> s r a t k", s=2, t=SLOTS, r=4)
        grad_raw, e_raw, back_raw = {}, {}, {}

        def load_grad(h, g):
            grad_raw[h, g] = sbuf("grad_raw", [P, TILES, W], BF16, GRAD_BUFS)
            nc.sync.dma_start(out=grad_raw[h, g][:], in_=grad_rows[:, TILES * h:TILES * (h + 1), W * g:W * (g + 1)])

        def load_e_codes(gp):
            e_raw[gp] = sbuf("e_raw%d" % gp, [P, 2, N // 2], I32)
            nc.sync.dma_start(out=e_raw[gp][:], in_=e_words[:, 2 * gp:2 * gp + 2, :])

        def load_e_scales():
            rows = basis_scales.bitcast(I32).rearrange("g (q r) n -> r q g n", r=4)
            for r in range(4):
                nc.sync.dma_start(out=scale_raw[:].bitcast(I32)[r:P:32, :, :], in_=rows[r])

        def load_by_direction(tile, vector):
            for r in range(4):
                nc.sync.dma_start(out=tile[r:P:4, :, 0:RUN],
                                  in_=vector.rearrange("(s a c) -> a s c", s=2, c=16)[:, :, r:r + RUN])

        def load_back(kh, s):
            back_raw[kh, s] = sbuf("back_raw%d%d" % (kh, s), [P, SLOTS, 2 * W], BF16)
            for r in range(4):
                nc.sync.dma_start(out=back_raw[kh, s][r:P:4, :, :],
                                  in_=back_rows[s, r][:, :, 2 * W * kh:2 * W * (kh + 1)])

        nc.vector.memset(scale_raw[:].bitcast(I32), 0)
        make_identity(nc, identity[:])

        load_grad(0, 0)
        nc.sync.dma_start(out=mu_col[:], in_=mu.rearrange("(p m) -> p m", m=2 * TILES))
        load_e_scales()
        load_grad(0, 1)
        load_e_codes(0)
        load_by_direction(lam_raw, lam)
        load_grad(0, 2)
        load_back(0, 0)
        load_e_codes(1)
        load_grad(0, 3)
        load_back(0, 1)
        load_grad(1, 0)
        load_grad(1, 1)
        load_by_direction(rad_raw, radius)

        rad = sbuf("rad", [P, 2, SLOTS], F32)
        ln_mu = sbuf("ln_mu", [P, M], F32)
        ln_lam = sbuf("ln_lam", [P, 2, SLOTS], F32)
        inv_lam = sbuf("inv_lam", [P, 2, SLOTS], F32)
        neg_rad = sbuf("neg_rad", [P, 2, SLOTS], F32)

        def logarithms():
            spread = bank(LOW + SLOTS - 1, [P, TILES, P])
            for w in range(TILES):
                nc.tensor.transpose(spread[:, w, :], mu_col[:].bitcast(F32)[:, w:w + 1].to_broadcast([P, P]), identity[:])
            nc.scalar.activation(out=ln_mu[:].rearrange("q (w e p) -> q w e p", w=TILES, e=2),
                                 in_=spread[:].bitcast(BF16).rearrange("q w (p e) -> q w e p", e=2), func=ACT.Ln)
            nc.scalar.activation(out=ln_lam[:], in_=lam_raw[:, :, 0:RUN:4], func=ACT.Ln)

        def invert_lam():
            nc.vector.reciprocal(out=inv_lam[:], in_=lam_raw[:, :, 0:RUN:4])

        def clip_bounds():
            nc.vector.tensor_copy(out=rad[:], in_=rad_raw[:, :, 0:RUN:4])
            nc.vector.tensor_scalar(out=neg_rad[:], in0=rad_raw[:, :, 0:RUN:4], scalar1=-1.0, scalar2=None, op0=ALU.mult)

        e_codes, e_scales, turned, grad_words, grad_mx, coef = {}, {}, {}, {}, {}, {}

        def sort_e_codes(s, gp):
            e_codes[s, gp] = sbuf("e_codes%d%d" % (s, gp), [P, 2, SLOTS, 2 * P], U8)
            nc.vector.tensor_copy(
                out=e_codes[s, gp][:].bitcast(I32).rearrange("p g t (a w) -> p g t a w", w=2),
                in_=e_raw[gp][:, :, W // 2 * s:W // 2 * (s + 1)].rearrange("p g (a t w) -> p g t a w", t=SLOTS, w=2))

        def sort_e_scales(s):
            e_scales[s] = sbuf("e_scales%d" % s, [P, 4, SLOTS, P], U8)
            nc.vector.tensor_copy(
                out=e_scales[s][:].bitcast(I32),
                in_=scale_raw[:].bitcast(I32)[:, :, W // 4 * s:W // 4 * (s + 1)].rearrange("p g (a t) -> p g t a", t=SLOTS))

        def turn(h, g, first_bank):
            pairs = grad_raw[h, g][:].bitcast(F32)
            for b in range(2):
                turned[h, g, b] = bank(first_bank + b, [P, 2, 2, P])
                for m in range(2):
                    for u in range(2):
                        nc.tensor.transpose(turned[h, g, b][:, m, u, :], pairs[:, 2 * b + m, u:W // 2:2], identity[:])

        def turn_out(h, g, copy, banks=(0, 1)):
            if banks[0] == 0:
                grad_words[h, g] = sbuf("grad_words", [P, SLOTS * W], BF16, TURNED_BUFS)
            dst = grad_words[h, g][:].bitcast(F32).rearrange("p (b m r u) -> p b m r u", b=2, m=2, u=2)
            for b in banks:
                copy(out=dst[:, b], in_=turned[h, g, b][:].rearrange("p m u r -> p m r u"))

        def quantise(name, words, fmt):
            codes = sbuf(name + "_codes", [P, W], U32)
            scales = sbuf(name + "_scales", [P, W], U8)
            nc.vector.quantize_mx(out=codes[:].bitcast(fmt), scales=scales[:], in_=words[:])
            return codes, scales

        def quantise_grad(h, g):
            grad_mx[h, g] = quantise("grad%d%d" % (h, g), grad_words[h, g], E4M3X4)

        def coef_passes(h, s, slots, groups, first_bank):
            for g in groups:
                for t in slots:
                    if g == 0:
                        coef[h, s, t] = bank(first_bank + t, [P, W])
                    codes, scales = grad_mx[h, g]
                    nc.tensor.matmul_mx(out=coef[h, s, t][:], lhsT=e_codes[s, g // 2][:, g % 2, t, :].bitcast(E2M1X4),
                                        lhsT_scale=e_scales[s][:, g, t, :], rhs=codes[:].bitcast(E4M3X4),
                                        rhs_scale=scales[:], start=(g == 0), stop=(g == 3))

        sig, quotient, z, z_words, z_mx, back_words, back_mx = {}, {}, {}, {}, {}, {}, {}

        def sigmoids(h, s, slots):
            for t in slots:
                sig[h, s, t] = sbuf("sig", [P, W], F32, SIG_BUFS)
                nc.scalar.activation(out=sig[h, s, t][:], in_=ln_mu[:, W * h:W * (h + 1)], func=ACT.Sigmoid,
                                     bias=ln_lam[:, s, t:t + 1], scale=-1.0)

        def divide(h, s, slots):
            for t in slots:
                quotient[h, s, t] = sbuf("quotient", [P, W], BF16, QUOTIENT_BUFS)
                nc.vector.scalar_tensor_tensor(out=quotient[h, s, t][:], in0=coef[h, s, t][:], scalar=inv_lam[:, s, t:t + 1],
                                               in1=sig[h, s, t][:], op0=ALU.mult, op1=ALU.mult)

        def clip(h, s):
            z[h, s] = sbuf("z", [P, SLOTS, W], BF16)
            for t in range(SLOTS):
                nc.vector.tensor_scalar(out=z[h, s][:, t, :], in0=quotient[h, s, t][:], scalar1=rad[:, s, t:t + 1],
                                        scalar2=neg_rad[:, s, t:t + 1], op0=ALU.min, op1=ALU.max)

        def lay_words(dst, src, copy):
            copy(out=dst.rearrange("p (c i t) -> p c t i", i=4, t=SLOTS), in_=src.rearrange("p t (c i) -> p c t i", i=4))

        def lay_z(h, s, copy):
            z_words[h, s] = sbuf("z_words", [P, SLOTS * W], BF16, Z_WORD_BUFS)
            lay_words(z_words[h, s][:], z[h, s][:], copy)

        def quantise_z(h, s):
            z_mx[h, s] = quantise("z%d%d" % (h, s), z_words[h, s], E5M2X4)

        def lay_back(kq, s, copy):
            back_words[kq, s] = sbuf("back_words", [P, SLOTS * W], BF16, BACK_WORD_BUFS)
            lay_words(back_words[kq, s][:], back_raw[kq // 2, s][:, :, W * (kq % 2):W * (kq % 2 + 1)], copy)

        def quantise_back(kq, s):
            back_mx[kq, s] = quantise("back%d%d" % (kq, s), back_words[kq, s], E4M3X4)

        def result_pair(pair, first_bank, share):
            staged = sbuf("staged", [P, 2, W], F32, STAGED_BUFS)
            for n, (m, kq) in enumerate(pair):
                cols = slice(P * (m % TILES), P * (m % TILES + 1))
                prod = bank(first_bank + n, [P, W])
                for s in range(2):
                    z_codes, z_scales = z_mx[m // TILES, s]
                    back_codes, back_scales = back_mx[kq, s]
                    nc.tensor.matmul_mx(out=prod[:], lhsT=z_codes[:, cols].bitcast(E5M2X4), lhsT_scale=z_scales[:, cols],
                                        rhs=back_codes[:].bitcast(E4M3X4), rhs_scale=back_scales[:],
                                        start=(s == 0), stop=(s == 1))
                if share and n == 1:
                    nc.vector.tensor_scalar(out=staged[:, n, :], in0=prod[:], scalar1=-1.0, scalar2=None, op0=ALU.mult)
                else:
                    nc.scalar.activation(out=staged[:, n, :], in_=prod[:], func=ACT.Copy, scale=-1.0)
            (m0, kq0), (m1, kq1) = pair
            if m0 == m1:
                nc.sync.dma_start(out=out_rows[:, m0, W * kq0:W * (kq1 + 1)], in_=staged[:].rearrange("p n w -> p (n w)"))
            else:
                nc.sync.dma_start(out=out_rows[:, m0:m1 + 1, W * kq0:W * (kq0 + 1)], in_=staged[:])

        def along_k(tiles, kh):
            return [((m, 2 * kh), (m, 2 * kh + 1)) for m in tiles]

        def along_m(h, kq):
            return [((m, kq), (m + 1, kq)) for m in range(TILES * h, TILES * (h + 1), 2)]

        every, early, late = range(4), (0, 1), (2, 3)

        logarithms()
        sort_e_scales(0)
        sort_e_scales(1)
        turn(0, 0, HIGH)
        turn(0, 1, HIGH + 2)
        load_grad(1, 2)
        load_grad(1, 3)
        load_back(1, 0)
        load_back(1, 1)
        turn_out(0, 0, on_vector)
        sort_e_codes(0, 0)
        quantise_grad(0, 0)
        turn_out(0, 1, on_vector, (0,))
        sort_e_codes(1, 0)
        turn_out(0, 1, on_vector, (1,))
        coef_passes(0, 0, every, (0,), LOW)
        invert_lam()
        quantise_grad(0, 1)
        lay_back(0, 0, on_vector)
        lay_back(1, 0, on_vector)
        sigmoids(0, 0, every)
        turn(0, 2, HIGH)
        turn_out(0, 2, on_scalar)
        coef_passes(0, 0, every, (1,), LOW)
        sort_e_codes(0, 1)
        quantise_grad(0, 2)
        sort_e_codes(1, 1)
        quantise_back(0, 0)
        sigmoids(0, 1, every)
        coef_passes(0, 1, early, early, HIGH)
        turn(0, 3, HIGH + 2)
        turn_out(0, 3, on_scalar)
        coef_passes(0, 0, every, (2,), LOW)
        quantise_back(1, 0)
        quantise_grad(0, 3)
        lay_back(0, 1, on_vector)
        coef_passes(0, 1, early, (2,), HIGH)
        coef_passes(0, 0, every, (3,), LOW)
        lay_back(1, 1, on_scalar)
        sigmoids(1, 0, early)
        divide(0, 0, every)
        coef_passes(0, 1, early, (3,), HIGH)

        turn(1, 0, LOW)
        turn_out(1, 0, on_scalar)
        sigmoids(1, 0, late)
        divide(0, 1, early)
        clip_bounds()
        quantise_grad(1, 0)
        coef_passes(0, 1, (2,), every, HIGH)
        clip(0, 0)
        divide(0, 1, (2,))
        lay_z(0, 0, on_vector)
        turn(1, 1, LOW + 2)
        turn_out(1, 1, on_scalar)
        sigmoids(1, 1, early)
        coef_passes(0, 1, (3,), every, HIGH)
        divide(0, 1, (3,))
        quantise_grad(1, 1)
        quantise_z(0, 0)
        clip(0, 1)
        turn(1, 2, LOW)
        turn_out(1, 2, on_scalar)
        sigmoids(1, 1, late)
        quantise_grad(1, 2)
        quantise_back(0, 1)

        coef_passes(1, 0, every, (0,), HIGH)
        turn(1, 3, LOW + 2)
        turn_out(1, 3, on_scalar)
        lay_back(2, 0, on_scalar)
        lay_back(2, 1, on_scalar)
        quantise_grad(1, 3)
        lay_z(0, 1, on_vector)
        quantise_back(1, 1)
        quantise_z(0, 1)
        coef_passes(1, 0, every, (1, 2, 3), HIGH)
        divide(1, 0, every)

        for t in early:
            coef_passes(1, 1, (t,), every, LOW)
        for n, pair in enumerate(along_k(early, 0)):
            result_pair(pair, HIGH + 2 * n, False)
        for t in late:
            coef_passes(1, 1, (t,), every, LOW)
        clip(1, 0)
        divide(1, 1, (0,))
        lay_z(1, 0, on_scalar)
        divide(1, 1, (1, 2))
        quantise_back(2, 0)
        divide(1, 1, (3,))
        quantise_back(2, 1)
        clip(1, 1)
        lay_z(1, 1, on_vector)
        quantise_z(1, 0)
        for n, pair in enumerate(along_k(late, 0) + along_m(0, 2)):
            result_pair(pair, (HIGH + 2 * n) % BANKS, False)
        quantise_z(1, 1)

        lay_back(3, 0, on_vector)
        lay_back(3, 1, on_vector)
        quantise_back(3, 0)
        quantise_back(3, 1)
        second_half = range(TILES, 2 * TILES)
        for n, pair in enumerate(along_k(second_half, 0) + along_m(0, 3) + along_k(second_half, 1)):
            result_pair(pair, (HIGH + 2 * n) % BANKS, n >= 2)
